import numpy as np
import ml_dtypes


def mxq(x, axis, fmt="e4m3"):
    dtype, down = {"e4m3": (ml_dtypes.float8_e4m3fn, 7), "e5m2": (ml_dtypes.float8_e5m2, 14)}[fmt]
    v = np.moveaxis(np.asarray(x, np.float32).astype(ml_dtypes.bfloat16).astype(np.float64), axis, -1)
    blocks = v.reshape(v.shape[:-1] + (-1, 32))
    amax = np.abs(blocks).max(-1, keepdims=True)
    byte = np.maximum(np.where(amax > 0, np.frexp(amax)[1] - 1 + 127, 0) - down, 1)
    scale = np.exp2(byte - 127.0)
    codes = (blocks / scale).astype(np.float32).astype(dtype).astype(np.float64)
    return np.moveaxis((codes * scale).reshape(v.shape), -1, axis)


WIDE = False


def mx_kscale(k):
    if not WIDE:
        return np.ones(k)
    levels = np.array([10, -10, 5, -5, 0])
    if k % 512:
        return np.exp2(np.random.permutation(np.resize(levels, k // 32))).repeat(32)
    a = np.empty((k // 512, 16))
    for p in range(k // 512):
        a[p, :8] = np.random.permutation(np.resize(levels, 8))
        for g in range(8):
            far = levels[np.abs(levels - a[p, g]) >= 10]
            a[p, g + 8] = far[np.random.randint(len(far))]
    return np.exp2(a.ravel()).repeat(32)


def f64(x):
    return np.asarray(x).astype(np.float64)


def striped(idx):
    return np.tile(np.asarray(idx).reshape(-1, 16).T, (8, 1)).astype(np.uint16)


def unstriped(offs):
    return offs[:16].T.reshape(-1).astype(np.int64)


E2M1 = np.array([0.0, 0.5, 1.0, 1.5, 2.0, 3.0, 4.0, 6.0, -0.0, -0.5, -1.0, -1.5, -2.0, -3.0, -4.0, -6.0])


def pack_weight(w, fmt):
    k, n = w.shape
    w = f64(np.asarray(w, np.float32).astype(ml_dtypes.bfloat16)).reshape(k // 32, 32, n)
    amax = np.abs(w).max(1)
    if fmt == "e4m3":
        byte = np.frexp(amax)[1] - 1 + 127 - 7
    else:
        mant, ex = np.frexp(amax / 6.0)
        byte = np.where(mant > 0.5, ex, ex - 1) + 127
    byte = np.clip(np.where(amax > 0, byte, 1), 1, 254)
    scaled = (w * np.exp2(127.0 - byte)[:, None, :]).reshape(k, n).astype(np.float32)
    by_word = np.ascontiguousarray(scaled.reshape(k // 512, 128, 4, n).transpose(0, 1, 3, 2))
    if fmt == "e4m3":
        words = by_word.astype(ml_dtypes.float8_e4m3fn).view(np.uint8)
    else:
        c = by_word.astype(ml_dtypes.float4_e2m1fn).view(np.uint8) & 0xF
        words = (c[..., 0::2] | (c[..., 1::2] << 4)).reshape(k // 512, 128, 2 * n)
    return np.ascontiguousarray(words), np.ascontiguousarray(byte.astype(np.uint8).reshape(k // 512, 16, n))


def unpack_weight(words, scales, fmt):
    g, _, n = scales.shape
    words = np.ascontiguousarray(words).reshape(g, 128, n, -1)
    if fmt == "e4m3":
        vals = words.view(ml_dtypes.float8_e4m3fn).astype(np.float64)
    else:
        nib = np.empty((g, 128, n, 4), np.uint8)
        nib[..., 0::2] = words & 0xF
        nib[..., 1::2] = words >> 4
        vals = E2M1[nib]
    vals = vals * np.repeat(np.exp2(scales.astype(np.float64) - 127.0), 8, axis=1)[..., None]
    return vals.transpose(0, 1, 3, 2).reshape(g * 512, n)


def sigmoid(v):
    return 1.0 / (1.0 + np.exp(-v))


def rot(x):
    y = x.reshape(-1, 2, x.shape[1])
    return np.stack([-y[:, 1], y[:, 0]], axis=1).reshape(x.shape)


K, R, F, T, J, U = 512, 512, 512, 2048, 256, 512


def setup_inputs():
    n = np.random.standard_normal
    idx = np.random.permutation(T)[:J]
    idx2 = np.random.randint(0, U, J)
    fk = mx_kscale(K)
    ff = mx_kscale(F)
    tabp = pack_weight(n((K, T)) / fk[:, None], "e4m3")
    return {
        "tab_words": tabp[0],
        "tab_scales": tabp[1],
        "w1": (n((K, R)) * 1 / np.sqrt(K) * fk[:, None]).astype(np.float32),
        "cosn": (np.repeat(np.round(np.cos(np.arange(R // 2)[:, None] * 0.11 + np.arange(U)[None] * 0.37) * 64) / 64, 2, axis=0)).astype(np.float32),
        "sinn": (np.repeat(np.round(np.sin(np.arange(R // 2)[:, None] * 0.11 + np.arange(U)[None] * 0.37) * 64) / 64, 2, axis=0)).astype(np.float32),
        "gain": (np.random.uniform(0.5, 1.5, (R, 1))).astype(np.float32),
        "wo": (n((F, R)) * 1 / np.sqrt(F) * ff[:, None]).astype(np.float32),
        "dy": (n((F, J)) / ff[:, None]).astype(np.float32),
        "og": (np.random.uniform(0.3, 1.0, (R, 1))).astype(np.float32),
        "base": (0.3 * n((R, J))).astype(np.float32),
        "offs": striped(idx),
        "offs2": striped(idx2),
    }


def reference(tab_words, tab_scales, w1, cosn, sinn, gain, wo, dy, og, base, offs, offs2):
    idx = unstriped(offs)
    idx2 = unstriped(offs2)
    tabu = unpack_weight(tab_words, tab_scales, "e4m3")
    w1q = mxq(f64(w1), 0, "e4m3")
    tabidxg = tabu[:, idx]
    a = w1q.T @ tabidxg
    o1 = rot(a)
    s = a * f64(cosn)[:, idx2] + o1 * f64(sinn)[:, idx2]
    s2 = s * f64(gain)
    woq = mxq(f64(wo), 0, "e4m3")
    dyq = mxq(f64(dy), 0, "e4m3")
    c0 = woq.T @ dyq
    ds2 = c0 * sigmoid(s2) * (1.0 + s2 * (1.0 - sigmoid(s2)))
    ds = ds2 * f64(gain)
    do1 = ds * f64(sinn)[:, idx2]
    odo1 = rot(do1)
    da = ds * f64(cosn)[:, idx2] - odo1
    hda = da * 2.0
    hodo1 = hda * (-1.0)
    ohodo1 = rot(hodo1)
    hdo1 = ohodo1 * (-1.0)
    hds = hda * f64(cosn)[:, idx2] + hdo1 * f64(sinn)[:, idx2]
    hds2 = hds * f64(gain)
    hs2 = hds2 * c0 * (1.0 + s2 * (1.0 - sigmoid(s2))) * sigmoid(s2) * (1.0 - sigmoid(s2)) + hds2 * c0 * sigmoid(s2) * (1.0 - sigmoid(s2)) + hds2 * c0 * sigmoid(s2) * s2 * (-1.0) * sigmoid(s2) * (1.0 - sigmoid(s2))
    hs = hs2 * f64(gain)
    ho1 = hs * f64(sinn)[:, idx2]
    oho1 = rot(ho1)
    ha = hs * f64(cosn)[:, idx2] - oho1
    y = ha * f64(og) + f64(base)
    return y

@@ -1,0 +1,214 @@
+from contextlib import ExitStack
+
+import concourse.mybir as mybir
+
+K, R, F, T, J, U = 512, 512, 512, 2048, 256, 512
+FLOPS = 2 * K * R * J + 2 * F * R * J
+
+F32 = mybir.dt.float32
+BF16 = mybir.dt.bfloat16
+I32 = mybir.dt.int32
+U32 = mybir.dt.uint32
+U16 = mybir.dt.uint16
+U8 = mybir.dt.uint8
+FP8X4 = mybir.dt.float8_e4m3fn_x4
+MULT = mybir.AluOpType.mult
+ADD = mybir.AluOpType.add
+ACT = mybir.ActivationFunctionType
+
+P = 128
+PACK = 4
+HALVES = 2
+HALF = R // HALVES
+
+
+def tile_attend_gpturned_kernel(tc, tab_words, tab_scales, w1, cosn, sinn, gain, wo, dy, og, base, offs, offs2, out):
+    nc = tc.nc
+    with ExitStack() as ctx:
+        keep = ctx.enter_context(tc.tile_pool(name="keep", bufs=1))
+        psum = ctx.enter_context(tc.psum_pool(name="psum", bufs=1))
+
+        def sb(name, shape, dtype=F32):
+            return keep.tile(shape, dtype, name=name, align_bytes=64)
+
+        def pair(name, q):
+            return sb("%s%d" % (name, q), [P, 2, J])
+
+        tab_bytes = sb("tab_bytes", [P, T], U8)
+        nc.vector.memset(tab_bytes[:].bitcast(I32), 0)
+        for quad in range(4):
+            nc.scalar.dma_start(
+                tab_bytes[32 * quad : 32 * quad + 4, :].bitcast(I32),
+                tab_scales[0, 4 * quad : 4 * quad + 4, :].bitcast(I32),
+            )
+        warm_in = sb("warm_in", [P, 1])
+        warm_out = sb("warm_out", [P, 1])
+        nc.gpsimd.memset(warm_in[:], 0.0)
+        nc.scalar.activation(warm_out[:], warm_in[:], ACT.Silu)
+
+        col_list = keep.tile([P, J // 16], U16, name="col_list")
+        angle_list = keep.tile([P, J // 16], U16, name="angle_list")
+        tab_codes = sb("tab_codes", [P, T], U32)
+        gains = sb("gains", [P, HALVES, 2])
+        out_gains = sb("out_gains", [P, HALVES, 2])
+        dy_raw = sb("dy_raw", [P, PACK, J])
+
+        def load_weight_half(name, w, q):
+            raw = sb("%s%d" % (name, q), [P, PACK, HALF])
+            nc.sync.dma_start(raw[:], w.rearrange("(p t) r -> p t r", t=PACK)[:, :, HALF * q : HALF * (q + 1)])
+            return raw
+
+        def load_angle_rows(name, table, q):
+            rows = sb("%s%d" % (name, q), [P, U])
+            nc.sync.dma_start(rows[:], table.rearrange("(q p e) u -> q e p u", q=HALVES, e=2)[q, 0])
+            return rows
+
+        def load_base(q):
+            rows = pair("base_rows", q)
+            nc.sync.dma_start(rows[:], base.rearrange("(q p e) j -> q p e j", q=HALVES, e=2)[q])
+            return rows
+
+        nc.sync.dma_start(angle_list[:], offs2)
+        cos0 = load_angle_rows("cos_rows", cosn, 0)
+        sin0 = load_angle_rows("sin_rows", sinn, 0)
+        nc.sync.dma_start(tab_codes[:].bitcast(I32), tab_words[0].rearrange("p n t -> p (n t)").bitcast(I32))
+        nc.sync.dma_start(col_list[:], offs)
+        nc.sync.dma_start(gains[:], gain.rearrange("(q p e) o -> p q (e o)", q=HALVES, e=2))
+        w1_0 = load_weight_half("w1_raw", w1, 0)
+        nc.sync.dma_start(dy_raw[:], dy.rearrange("(p t) j -> p t j", t=PACK))
+        wo_0 = load_weight_half("wo_raw", wo, 0)
+        cos1 = load_angle_rows("cos_rows", cosn, 1)
+        sin1 = load_angle_rows("sin_rows", sinn, 1)
+        w1_1 = load_weight_half("w1_raw", w1, 1)
+        nc.sync.dma_start(out_gains[:], og.rearrange("(q p e) o -> p q (e o)", q=HALVES, e=2))
+        wo_1 = load_weight_half("wo_raw", wo, 1)
+        base_rows = [load_base(q) for q in range(HALVES)]
+
+        def gather_angles(q, cos_rows, sin_rows):
+            cs = pair("cs", q)
+            nc.vector.tensor_copy(cs[:, 0, :], cos_rows[:].indirect(angle_list[:]))
+            nc.vector.tensor_copy(cs[:, 1, :], sin_rows[:].indirect(angle_list[:]))
+            return cs
+
+        def scaled_angles(q, cs):
+            cs_sq = pair("cs_sq", q)
+            norm = sb("norm%d" % q, [P, J])
+            csn = pair("csn", q)
+            nc.scalar.activation(cs_sq[:], cs[:], ACT.Square)
+            nc.vector.tensor_tensor(norm[:], cs_sq[:, 0, :], cs_sq[:, 1, :], ADD)
+            nc.vector.tensor_tensor(csn[:], cs[:], norm[:].unsqueeze(1).to_broadcast([P, 2, J]), MULT)
+            return csn
+
+        def quantise(name, grouped, width):
+            codes = sb(name + "_codes", [P, width], U32)
+            scales = sb(name + "_scales", [P, width], U8)
+            nc.vector.quantize_mx(out=codes[:].bitcast(FP8X4), scales=scales[:], in_=grouped[:])
+            return codes, scales
+
+        def cast_weight(name, raw):
+            grouped = sb(name + "_grouped", [P, HALF * PACK], BF16)
+            nc.scalar.copy(
+                grouped[:].rearrange("p (e b i t) -> p b t i e", e=2, i=2, t=PACK),
+                raw[:].rearrange("p t (b i e) -> p b t i e", i=2, e=2),
+            )
+            return grouped
+
+        def product(name, stationary, moving):
+            acc = psum.tile([P, 2, J], F32, name=name)
+            for e in range(2):
+                cols = slice(P * e, P * (e + 1))
+                nc.tensor.matmul_mx(
+                    out=acc[:, e, :],
+                    lhsT=stationary[0][:, cols].bitcast(FP8X4),
+                    lhsT_scale=stationary[1][:, cols],
+                    rhs=moving[0][:].bitcast(FP8X4),
+                    rhs_scale=moving[1][:],
+                    start=True,
+                    stop=True,
+                )
+            return acc
+
+        half_gain = sb("half_gain", [P, HALVES, 2])
+        neg_half_gain = sb("neg_half_gain", [P, HALVES, 2])
+        gain_sq = sb("gain_sq", [P, HALVES, 2])
+        cube = sb("cube", [P, HALVES, 2])
+        own = sb("own", [P, HALVES, 2])
+        cross = sb("cross", [P, HALVES, 2])
+
+        def turn(q, a, cs):
+            t1, t2, h = pair("t1", q), pair("t2", q), pair("h", q)
+            nc.vector.scalar_tensor_tensor(t1[:, 0, :], a[:, 0, :], half_gain[:, q, 0:1], cs[:, 0, :], MULT, MULT)
+            nc.vector.scalar_tensor_tensor(t2[:, 0, :], a[:, 1, :], neg_half_gain[:, q, 0:1], cs[:, 1, :], MULT, MULT)
+            nc.vector.scalar_tensor_tensor(t1[:, 1, :], a[:, 1, :], half_gain[:, q, 1:2], cs[:, 0, :], MULT, MULT)
+            nc.vector.scalar_tensor_tensor(t2[:, 1, :], a[:, 0, :], half_gain[:, q, 1:2], cs[:, 1, :], MULT, MULT)
+            for e in range(2):
+                nc.vector.tensor_tensor(h[:, e, :], t1[:, e, :], t2[:, e, :], ADD)
+            th, m = pair("th", q), pair("m", q)
+            nc.scalar.activation(m[:], h[:], ACT.Silu, scale=-2.0)
+            nc.scalar.activation(th[:], h[:], ACT.Tanh)
+            return h, th, m
+
+        def lead_square(q, th, c0):
+            lead, lead_sq = pair("lead", q), pair("lead_sq", q)
+            nc.vector.scalar_tensor_tensor(lead[:], th[:], 1.0, c0[:], ADD, MULT)
+            nc.scalar.activation(lead_sq[:], lead[:], ACT.Square)
+            return lead_sq
+
+        def curvature(q, h, th, m):
+            z0, z1, z2 = pair("z0", q), pair("z1", q), pair("z2", q)
+            for e in range(2):
+                nc.vector.scalar_tensor_tensor(z0[:, e, :], h[:, e, :], -1.0, m[:, e, :], ADD, ADD)
+            for e in range(2):
+                nc.vector.scalar_tensor_tensor(z1[:, e, :], m[:, e, :], -1.0, z0[:, e, :], ADD, MULT)
+            for e in range(2):
+                nc.vector.scalar_tensor_tensor(z2[:, e, :], th[:, e, :], -1.0, z1[:, e, :], ADD, MULT)
+            return z2
+
+        def turn_back(q, z2, lead_sq, csn):
+            z3, u1, u2, v, y = pair("z3", q), pair("u1", q), pair("u2", q), pair("v", q), pair("y", q)
+            for e in range(2):
+                nc.vector.tensor_tensor(z3[:, e, :], z2[:, e, :], lead_sq[:, e, :], MULT)
+            for e in range(2):
+                nc.vector.scalar_tensor_tensor(u1[:, e, :], z3[:, e, :], own[:, q, e : e + 1], csn[:, 0, :], MULT, MULT)
+            for e in range(2):
+                nc.vector.scalar_tensor_tensor(u2[:, e, :], z3[:, 1 - e, :], cross[:, q, e : e + 1], csn[:, 1, :], MULT, MULT)
+            for e in range(2):
+                nc.vector.tensor_tensor(v[:, e, :], u1[:, e, :], base_rows[q][:, e, :], ADD)
+            for e in range(2):
+                nc.vector.tensor_tensor(y[:, e, :], v[:, e, :], u2[:, e, :], ADD)
+                nc.sync.dma_start(out.rearrange("(q p e) j -> q e p j", q=HALVES, e=2)[q, e], y[:, e, :])
+
+        cs0 = gather_angles(0, cos0, sin0)
+        csn0 = scaled_angles(0, cs0)
+        tab_g = sb("tab_g", [P, J], U32)
+        tab_gs = sb("tab_gs", [P, J], U8)
+        nc.vector.tensor_copy(tab_gs[:], tab_bytes[:].indirect(col_list[:]))
+        nc.vector.tensor_copy(tab_g[:], tab_codes[:].indirect(col_list[:]))
+        nc.vector.tensor_scalar(half_gain[:], gains[:], 0.5, None, MULT)
+        nc.vector.tensor_scalar(neg_half_gain[:], gains[:], -0.5, None, MULT)
+        nc.vector.tensor_tensor(gain_sq[:], gains[:], gains[:], MULT)
+        a0 = product("a0", quantise("w1_0", cast_weight("w1_0", w1_0), HALF), (tab_g, tab_gs))
+        nc.vector.tensor_tensor(cube[:], gain_sq[:], neg_half_gain[:], MULT)
+
+        dy_grouped = sb("dy_grouped", [P, J * PACK], BF16)
+        nc.scalar.copy(
+            dy_grouped[:].rearrange("p (b i t) -> p b t i", i=4, t=PACK),
+            dy_raw[:].rearrange("p t (b i) -> p b t i", i=4),
+        )
+        h0, th0, m0 = turn(0, a0, cs0)
+        dy_q = quantise("dy", dy_grouped, J)
+        c0_0 = product("c0_0", quantise("wo_0", cast_weight("wo_0", wo_0), HALF), dy_q)
+        cs1 = gather_angles(1, cos1, sin1)
+        sq0 = lead_square(0, th0, c0_0)
+        a1 = product("a1", quantise("w1_1", cast_weight("w1_1", w1_1), HALF), (tab_g, tab_gs))
+        z2_0 = curvature(0, h0, th0, m0)
+        nc.vector.tensor_tensor(own[:], cube[:], out_gains[:], MULT)
+        nc.vector.tensor_tensor(cross[:, :, 0], cube[:, :, 1], out_gains[:, :, 0], MULT)
+        nc.vector.scalar_tensor_tensor(cross[:, :, 1], cube[:, :, 0], -1.0, out_gains[:, :, 1], MULT, MULT)
+        h1, th1, m1 = turn(1, a1, cs1)
+        c0_1 = product("c0_1", quantise("wo_1", cast_weight("wo_1", wo_1), HALF), dy_q)
+        turn_back(0, z2_0, sq0, csn0)
+        csn1 = scaled_angles(1, cs1)
+        sq1 = lead_square(1, th1, c0_1)
+        z2_1 = curvature(1, h1, th1, m1)
+        turn_back(1, z2_1, sq1, csn1)

@@ -1,6 +1,7 @@
 from contextlib import ExitStack
 
 import concourse.mybir as mybir
+from concourse.masks import make_identity
 
 K, R, F, T, J, U = 512, 512, 512, 2048, 256, 512
 FLOPS = 2 * K * R * J + 2 * F * R * J
@@ -28,23 +29,26 @@ def tile_attend_gpturned_kernel(tc, tab_words, tab_scales, w1, cosn, sinn, gain,
         keep = ctx.enter_context(tc.tile_pool(name="keep", bufs=1))
         psum = ctx.enter_context(tc.psum_pool(name="psum", bufs=1))
 
-        def sb(name, shape, dtype=F32):
-            return keep.tile(shape, dtype, name=name, align_bytes=64)
+        def sb(name, shape, dtype=F32, after=None):
+            return keep.tile(shape, dtype, name=name, tag=after or name, align_bytes=64)
 
-        def pair(name, q):
+        def by_feature(name, q):
             return sb("%s%d" % (name, q), [P, 2, J])
+
+        def by_slot(name, q, after=None):
+            return sb("%s%d" % (name, q), [P, 2, 2 * P], F32, after)
+
+        def bank(name, tag):
+            return psum.tile([P, 2, 2 * P], F32, name=name, tag=tag)
 
         tab_bytes = sb("tab_bytes", [P, T], U8)
         nc.vector.memset(tab_bytes[:].bitcast(I32), 0)
-        for quad in range(4):
-            nc.scalar.dma_start(
-                tab_bytes[32 * quad : 32 * quad + 4, :].bitcast(I32),
-                tab_scales[0, 4 * quad : 4 * quad + 4, :].bitcast(I32),
-            )
         warm_in = sb("warm_in", [P, 1])
         warm_out = sb("warm_out", [P, 1])
         nc.gpsimd.memset(warm_in[:], 0.0)
         nc.scalar.activation(warm_out[:], warm_in[:], ACT.Silu)
+        identity = sb("identity", [P, P])
+        make_identity(nc, identity[:])
 
         col_list = keep.tile([P, J // 16], U16, name="col_list")
         angle_list = keep.tile([P, J // 16], U16, name="angle_list")
@@ -64,61 +68,91 @@ def tile_attend_gpturned_kernel(tc, tab_words, tab_scales, w1, cosn, sinn, gain,
             return rows
 
         def load_base(q):
-            rows = pair("base_rows", q)
+            rows = by_feature("base_rows", q)
             nc.sync.dma_start(rows[:], base.rearrange("(q p e) j -> q p e j", q=HALVES, e=2)[q])
             return rows
 
         nc.sync.dma_start(angle_list[:], offs2)
-        cos0 = load_angle_rows("cos_rows", cosn, 0)
-        sin0 = load_angle_rows("sin_rows", sinn, 0)
-        nc.sync.dma_start(tab_codes[:].bitcast(I32), tab_words[0].rearrange("p n t -> p (n t)").bitcast(I32))
+        cos_rows, sin_rows = [], []
+        sin_rows.append(load_angle_rows("sin_rows", sinn, 0))
+        cos_rows.append(load_angle_rows("cos_rows", cosn, 0))
+        sin_rows.append(load_angle_rows("sin_rows", sinn, 1))
+        cos_rows.append(load_angle_rows("cos_rows", cosn, 1))
+        w1_raw = [load_weight_half("w1_raw", w1, 0)]
         nc.sync.dma_start(col_list[:], offs)
+        for quad in range(4):
+            nc.sync.dma_start(
+                tab_bytes[32 * quad : 32 * quad + 4, :].bitcast(I32),
+                tab_scales[0, 4 * quad : 4 * quad + 4, :].bitcast(I32),
+            )
+        nc.sync.dma_start(tab_codes[:].bitcast(I32), tab_words[0].rearrange("p n t -> p (n t)").bitcast(I32))
         nc.sync.dma_start(gains[:], gain.rearrange("(q p e) o -> p q (e o)", q=HALVES, e=2))
-        w1_0 = load_weight_half("w1_raw", w1, 0)
+        w1_raw.append(load_weight_half("w1_raw", w1, 1))
         nc.sync.dma_start(dy_raw[:], dy.rearrange("(p t) j -> p t j", t=PACK))
-        wo_0 = load_weight_half("wo_raw", wo, 0)
-        cos1 = load_angle_rows("cos_rows", cosn, 1)
-        sin1 = load_angle_rows("sin_rows", sinn, 1)
-        w1_1 = load_weight_half("w1_raw", w1, 1)
+        wo_raw = [load_weight_half("wo_raw", wo, q) for q in range(HALVES)]
         nc.sync.dma_start(out_gains[:], og.rearrange("(q p e) o -> p q (e o)", q=HALVES, e=2))
-        wo_1 = load_weight_half("wo_raw", wo, 1)
         base_rows = [load_base(q) for q in range(HALVES)]
 
-        def gather_angles(q, cos_rows, sin_rows):
-            cs = pair("cs", q)
-            nc.vector.tensor_copy(cs[:, 0, :], cos_rows[:].indirect(angle_list[:]))
-            nc.vector.tensor_copy(cs[:, 1, :], sin_rows[:].indirect(angle_list[:]))
-            return cs
+        half_gain = sb("half_gain", [P, HALVES, 2])
+        gain_sq = sb("gain_sq", [P, HALVES, 2])
+        cube = sb("cube", [P, HALVES, 2])
+        neg_cube = sb("neg_cube", [P, HALVES])
 
-        def scaled_angles(q, cs):
-            cs_sq = pair("cs_sq", q)
+        def gather_angles(q, after=None):
+            scs = sb("scs%d" % q, [P, 3, J], F32, after)
+            nc.vector.tensor_copy(scs[:, 0, :], sin_rows[q][:].indirect(angle_list[:]))
+            nc.vector.tensor_copy(scs[:, 1, :], cos_rows[q][:].indirect(angle_list[:]))
+            squares = by_feature("squares", q)
+            nc.scalar.activation(scs[:, 2, :], scs[:, 0, :], ACT.Copy, scale=-1.0)
+            nc.scalar.activation(squares[:], scs[:, 0:2, :], ACT.Square)
+            return scs, squares
+
+        def planes(scs, e):
+            return scs[:, 1 - e : 3 - e, :]
+
+        def angle_norm(q, squares):
             norm = sb("norm%d" % q, [P, J])
-            csn = pair("csn", q)
-            nc.scalar.activation(cs_sq[:], cs[:], ACT.Square)
-            nc.vector.tensor_tensor(norm[:], cs_sq[:, 0, :], cs_sq[:, 1, :], ADD)
-            nc.vector.tensor_tensor(csn[:], cs[:], norm[:].unsqueeze(1).to_broadcast([P, 2, J]), MULT)
-            return csn
+            nc.vector.tensor_tensor(norm[:], squares[:, 0, :], squares[:, 1, :], ADD)
+            return norm
 
-        def quantise(name, grouped, width):
-            codes = sb(name + "_codes", [P, width], U32)
+        def normed_angles(q, scs, norm, after):
+            normed = sb("normed%d" % q, [P, 2, J], F32, after)
+            nc.vector.tensor_tensor(normed[:], scs[:, 0:2, :], norm[:].unsqueeze(1).to_broadcast([P, 2, J]), MULT)
+            return normed
+
+        def back_tables(q, normed, after=None):
+            table = sb("table%d" % q, [P, 2, 2, J], F32, after)
+            nc.scalar.activation(table[:, 0, 0, :], normed[:, 1, :], ACT.Copy, scale=cube[:, q, 0:1])
+            nc.scalar.activation(table[:, 0, 1, :], normed[:, 0, :], ACT.Copy, scale=neg_cube[:, q : q + 1])
+            nc.scalar.activation(table[:, 1], normed[:], ACT.Copy, scale=cube[:, q, 1:2])
+            turned = []
+            for jb in range(2):
+                dst = psum.tile([P, 2, 2, P], F32, name="table_t%d%d" % (q, jb))
+                for e in range(2):
+                    for to in range(2):
+                        nc.tensor.transpose(dst[:, e, to, :], table[:, e, to, P * jb : P * (jb + 1)], identity[:])
+                turned.append(dst)
+            return turned
+
+        def quantise(name, grouped, width, after=None):
+            codes = sb(name + "_codes", [P, width], U32, after)
             scales = sb(name + "_scales", [P, width], U8)
             nc.vector.quantize_mx(out=codes[:].bitcast(FP8X4), scales=scales[:], in_=grouped[:])
             return codes, scales
 
-        def cast_weight(name, raw):
-            grouped = sb(name + "_grouped", [P, HALF * PACK], BF16)
+        def cast_weight(name, raw, after):
+            grouped = sb(name + "_grouped", [P, HALF * PACK], BF16, after)
             nc.scalar.copy(
                 grouped[:].rearrange("p (e b i t) -> p b t i e", e=2, i=2, t=PACK),
                 raw[:].rearrange("p t (b i e) -> p b t i e", i=2, e=2),
             )
             return grouped
 
-        def product(name, stationary, moving):
-            acc = psum.tile([P, 2, J], F32, name=name)
-            for e in range(2):
-                cols = slice(P * e, P * (e + 1))
+        def product(acc, stationary, moving):
+            for block in range(2):
+                cols = slice(P * block, P * (block + 1))
                 nc.tensor.matmul_mx(
-                    out=acc[:, e, :],
+                    out=acc[:, block, :],
                     lhsT=stationary[0][:, cols].bitcast(FP8X4),
                     lhsT_scale=stationary[1][:, cols],
                     rhs=moving[0][:].bitcast(FP8X4),
@@ -128,87 +162,111 @@ def tile_attend_gpturned_kernel(tc, tab_words, tab_scales, w1, cosn, sinn, gain,
                 )
             return acc
 
-        half_gain = sb("half_gain", [P, HALVES, 2])
-        neg_half_gain = sb("neg_half_gain", [P, HALVES, 2])
-        gain_sq = sb("gain_sq", [P, HALVES, 2])
-        cube = sb("cube", [P, HALVES, 2])
-        own = sb("own", [P, HALVES, 2])
-        cross = sb("cross", [P, HALVES, 2])
+        def sum_turned(dst, first, second):
+            nc.tensor.matmul(dst, first, identity[:], start=True, stop=False, is_transpose=True)
+            nc.tensor.matmul(dst, second, identity[:], start=False, stop=True, is_transpose=True)
 
-        def turn(q, a, cs):
-            t1, t2, h = pair("t1", q), pair("t2", q), pair("h", q)
-            nc.vector.scalar_tensor_tensor(t1[:, 0, :], a[:, 0, :], half_gain[:, q, 0:1], cs[:, 0, :], MULT, MULT)
-            nc.vector.scalar_tensor_tensor(t2[:, 0, :], a[:, 1, :], neg_half_gain[:, q, 0:1], cs[:, 1, :], MULT, MULT)
-            nc.vector.scalar_tensor_tensor(t1[:, 1, :], a[:, 1, :], half_gain[:, q, 1:2], cs[:, 0, :], MULT, MULT)
-            nc.vector.scalar_tensor_tensor(t2[:, 1, :], a[:, 0, :], half_gain[:, q, 1:2], cs[:, 1, :], MULT, MULT)
+        def turn_terms(q, a, scs, after=None):
+            terms = sb("terms%d" % q, [P, 2, 2, J], F32, after)
             for e in range(2):
-                nc.vector.tensor_tensor(h[:, e, :], t1[:, e, :], t2[:, e, :], ADD)
-            th, m = pair("th", q), pair("m", q)
+                nc.vector.scalar_tensor_tensor(terms[:, e], a[:], half_gain[:, q, e : e + 1], planes(scs, e), MULT, MULT)
+            return terms
+
+        def turn_sum(h, terms, e):
+            for jb in range(2):
+                slots = slice(P * jb, P * (jb + 1))
+                sum_turned(h[:, jb, P * e : P * (e + 1)], terms[:, e, 0, slots], terms[:, e, 1, slots])
+
+        def activate(q, h, after):
+            th, m = by_slot("th", q), by_slot("m", q, after)
             nc.scalar.activation(m[:], h[:], ACT.Silu, scale=-2.0)
             nc.scalar.activation(th[:], h[:], ACT.Tanh)
-            return h, th, m
+            return th, m
 
         def lead_square(q, th, c0):
-            lead, lead_sq = pair("lead", q), pair("lead_sq", q)
+            lead, lead_sq = by_slot("lead", q), by_slot("lead_sq", q)
             nc.vector.scalar_tensor_tensor(lead[:], th[:], 1.0, c0[:], ADD, MULT)
             nc.scalar.activation(lead_sq[:], lead[:], ACT.Square)
             return lead_sq
 
-        def curvature(q, h, th, m):
-            z0, z1, z2 = pair("z0", q), pair("z1", q), pair("z2", q)
-            for e in range(2):
-                nc.vector.scalar_tensor_tensor(z0[:, e, :], h[:, e, :], -1.0, m[:, e, :], ADD, ADD)
-            for e in range(2):
-                nc.vector.scalar_tensor_tensor(z1[:, e, :], m[:, e, :], -1.0, z0[:, e, :], ADD, MULT)
-            for e in range(2):
-                nc.vector.scalar_tensor_tensor(z2[:, e, :], th[:, e, :], -1.0, z1[:, e, :], ADD, MULT)
-            return z2
+        def shifted(name, q, first, op, second, after=None):
+            z = by_slot(name, q, after)
+            nc.vector.scalar_tensor_tensor(z[:], first[:], -1.0, second[:], ADD, op)
+            return z
 
-        def turn_back(q, z2, lead_sq, csn):
-            z3, u1, u2, v, y = pair("z3", q), pair("u1", q), pair("u2", q), pair("v", q), pair("y", q)
+        def weigh(q, z2, lead_sq):
+            z3 = by_slot("z3", q)
+            nc.vector.tensor_tensor(z3[:], z2[:], lead_sq[:], MULT)
+            return z3
+
+        def turn_back(q, z3, tables):
+            ha = bank("ha%d" % q, "h_ha%d" % q)
+            for jb in range(2):
+                sent = sb("sent%d%d" % (q, jb), [P, 2, 2, P])
+                source = z3[:, jb, :].rearrange("s (e p) -> s e p", e=2).unsqueeze(2).to_broadcast([P, 2, 2, P])
+                nc.vector.tensor_tensor(sent[:], tables[jb][:], source, MULT)
+                for to in range(2):
+                    sum_turned(ha[:, to, P * jb : P * (jb + 1)], sent[:, 0, to, :], sent[:, 1, to, :])
+            return ha
+
+        def finish(q, ha):
+            y = by_feature("y", q)
             for e in range(2):
-                nc.vector.tensor_tensor(z3[:, e, :], z2[:, e, :], lead_sq[:, e, :], MULT)
-            for e in range(2):
-                nc.vector.scalar_tensor_tensor(u1[:, e, :], z3[:, e, :], own[:, q, e : e + 1], csn[:, 0, :], MULT, MULT)
-            for e in range(2):
-                nc.vector.scalar_tensor_tensor(u2[:, e, :], z3[:, 1 - e, :], cross[:, q, e : e + 1], csn[:, 1, :], MULT, MULT)
-            for e in range(2):
-                nc.vector.tensor_tensor(v[:, e, :], u1[:, e, :], base_rows[q][:, e, :], ADD)
-            for e in range(2):
-                nc.vector.tensor_tensor(y[:, e, :], v[:, e, :], u2[:, e, :], ADD)
+                nc.vector.scalar_tensor_tensor(y[:, e, :], ha[:, e, :], out_gains[:, q, e : e + 1], base_rows[q][:, e, :], MULT, ADD)
                 nc.sync.dma_start(out.rearrange("(q p e) j -> q e p j", q=HALVES, e=2)[q, e], y[:, e, :])
 
-        cs0 = gather_angles(0, cos0, sin0)
-        csn0 = scaled_angles(0, cs0)
-        tab_g = sb("tab_g", [P, J], U32)
-        tab_gs = sb("tab_gs", [P, J], U8)
+        angles0 = gather_angles(0)
+        angles1 = gather_angles(1)
+        norm0 = angle_norm(0, angles0[1])
+        w1_g0 = cast_weight("w1_0", w1_raw[0], "cos_rows1")
+        tab_gs = sb("tab_gs", [P, J], U8, "squares0")
         nc.vector.tensor_copy(tab_gs[:], tab_bytes[:].indirect(col_list[:]))
+        norm1 = angle_norm(1, angles1[1])
+        w1_q0 = quantise("w1_0", w1_g0, HALF, "tab_bytes")
+        tab_g = sb("tab_g", [P, J], U32, "squares1")
         nc.vector.tensor_copy(tab_g[:], tab_codes[:].indirect(col_list[:]))
-        nc.vector.tensor_scalar(half_gain[:], gains[:], 0.5, None, MULT)
-        nc.vector.tensor_scalar(neg_half_gain[:], gains[:], -0.5, None, MULT)
-        nc.vector.tensor_tensor(gain_sq[:], gains[:], gains[:], MULT)
-        a0 = product("a0", quantise("w1_0", cast_weight("w1_0", w1_0), HALF), (tab_g, tab_gs))
-        nc.vector.tensor_tensor(cube[:], gain_sq[:], neg_half_gain[:], MULT)
-
-        dy_grouped = sb("dy_grouped", [P, J * PACK], BF16)
+        a0 = product(bank("a0", "a_c0"), w1_q0, (tab_g, tab_gs))
+        nc.scalar.activation(half_gain[:], gains[:], ACT.Copy, scale=0.5)
+        nc.scalar.activation(gain_sq[:], gains[:], ACT.Square)
+        normed0 = normed_angles(0, angles0[0], norm0, "tab_codes")
+        normed1 = normed_angles(1, angles1[0], norm1, "norm0")
+        nc.vector.scalar_tensor_tensor(cube[:], gain_sq[:], -0.5, gains[:], MULT, MULT)
+        nc.vector.scalar_tensor_tensor(neg_cube[:], gain_sq[:, :, 0], 0.5, gains[:, :, 0], MULT, MULT)
+        w1_g1 = cast_weight("w1_1", w1_raw[1], "w1_raw0")
+        a1 = product(bank("a1", "a_c1"), quantise("w1_1", w1_g1, HALF, "norm1"), (tab_g, tab_gs))
+        dy_grouped = sb("dy_grouped", [P, J * PACK], BF16, "w1_raw1")
         nc.scalar.copy(
             dy_grouped[:].rearrange("p (b i t) -> p b t i", i=4, t=PACK),
             dy_raw[:].rearrange("p t (b i) -> p b t i", i=4),
         )
-        h0, th0, m0 = turn(0, a0, cs0)
-        dy_q = quantise("dy", dy_grouped, J)
-        c0_0 = product("c0_0", quantise("wo_0", cast_weight("wo_0", wo_0), HALF), dy_q)
-        cs1 = gather_angles(1, cos1, sin1)
+        wo_g0 = cast_weight("wo_0", wo_raw[0], "dy_raw")
+        terms0 = turn_terms(0, a0, angles0[0], "w1_raw0")
+        h0 = bank("h0", "h_ha0")
+        for e in range(2):
+            turn_sum(h0, terms0, e)
+        terms1 = turn_terms(1, a1, angles1[0])
+        h1 = bank("h1", "h_ha1")
+        for e in range(2):
+            turn_sum(h1, terms1, e)
+        th0, m0 = activate(0, h0, "wo_raw0")
+        wo_g1 = cast_weight("wo_1", wo_raw[1], "sin_rows0")
+        th1, m1 = activate(1, h1, "wo_raw1")
+        dy_q = quantise("dy", dy_grouped, J, "scs0")
+        c0_0 = product(bank("c0_0", "a_c0"), dy_q, quantise("wo_0", wo_g0, HALF, "scs1"))
+        z0_0 = shifted("z0", 0, h0, ADD, m0, "dy_raw")
         sq0 = lead_square(0, th0, c0_0)
-        a1 = product("a1", quantise("w1_1", cast_weight("w1_1", w1_1), HALF), (tab_g, tab_gs))
-        z2_0 = curvature(0, h0, th0, m0)
-        nc.vector.tensor_tensor(own[:], cube[:], out_gains[:], MULT)
-        nc.vector.tensor_tensor(cross[:, :, 0], cube[:, :, 1], out_gains[:, :, 0], MULT)
-        nc.vector.scalar_tensor_tensor(cross[:, :, 1], cube[:, :, 0], -1.0, out_gains[:, :, 1], MULT, MULT)
-        h1, th1, m1 = turn(1, a1, cs1)
-        c0_1 = product("c0_1", quantise("wo_1", cast_weight("wo_1", wo_1), HALF), dy_q)
-        turn_back(0, z2_0, sq0, csn0)
-        csn1 = scaled_angles(1, cs1)
+        z1_0 = shifted("z1", 0, m0, MULT, z0_0)
+        c0_1 = product(bank("c0_1", "a_c1"), dy_q, quantise("wo_1", wo_g1, HALF))
+        z2_0 = shifted("z2", 0, th0, MULT, z1_0)
+        tables0 = back_tables(0, normed0, "dy_raw")
+        z0_1 = shifted("z0", 1, h1, ADD, m1)
+        z3_0 = weigh(0, z2_0, sq0)
         sq1 = lead_square(1, th1, c0_1)
-        z2_1 = curvature(1, h1, th1, m1)
-        turn_back(1, z2_1, sq1, csn1)
+        tables1 = back_tables(1, normed1, "sin_rows0")
+        z1_1 = shifted("z1", 1, m1, MULT, z0_1)
+        z2_1 = shifted("z2", 1, th1, MULT, z1_1)
+        ha0 = turn_back(0, z3_0, tables0)
+        z3_1 = weigh(1, z2_1, sq1)
+        ha1 = turn_back(1, z3_1, tables1)
+        finish(0, ha0)
+        finish(1, ha1)

@@ -196,23 +196,26 @@ def tile_attend_gpturned_kernel(tc, tab_words, tab_scales, w1, cosn, sinn, gain,
 
         def weigh(q, z2, lead_sq):
             z3 = by_slot("z3", q)
-            nc.vector.tensor_tensor(z3[:], z2[:], lead_sq[:], MULT)
+            nc.gpsimd.tensor_tensor(z3[:], z2[:], lead_sq[:], MULT)
             return z3
 
         def turn_back(q, z3, tables):
-            ha = bank("ha%d" % q, "h_ha%d" % q)
+            ha = [psum.tile([P, J], F32, name="ha%d%d" % (q, to), tag=tag % q) for to, tag in enumerate(("h_ha%d", "a_c%d"))]
             for jb in range(2):
                 sent = sb("sent%d%d" % (q, jb), [P, 2, 2, P])
-                source = z3[:, jb, :].rearrange("s (e p) -> s e p", e=2).unsqueeze(2).to_broadcast([P, 2, 2, P])
-                nc.vector.tensor_tensor(sent[:], tables[jb][:], source, MULT)
+                source = z3[:, jb, :].rearrange("s (e p) -> s e p", e=2)
+                if jb == 0:
+                    nc.vector.tensor_tensor(sent[:], tables[jb][:], source.unsqueeze(2).to_broadcast([P, 2, 2, P]), MULT)
                 for to in range(2):
-                    sum_turned(ha[:, to, P * jb : P * (jb + 1)], sent[:, 0, to, :], sent[:, 1, to, :])
+                    if jb == 1:
+                        nc.vector.tensor_tensor(sent[:, :, to, :], tables[jb][:, :, to, :], source, MULT)
+                    sum_turned(ha[to][:, P * jb : P * (jb + 1)], sent[:, 0, to, :], sent[:, 1, to, :])
             return ha
 
-        def finish(q, ha):
-            y = by_feature("y", q)
+        def finish(q, ha, after=None):
+            y = sb("y%d" % q, [P, 2, J], F32, after)
             for e in range(2):
-                nc.vector.scalar_tensor_tensor(y[:, e, :], ha[:, e, :], out_gains[:, q, e : e + 1], base_rows[q][:, e, :], MULT, ADD)
+                nc.vector.scalar_tensor_tensor(y[:, e, :], ha[e][:], out_gains[:, q, e : e + 1], base_rows[q][:, e, :], MULT, ADD)
                 nc.sync.dma_start(out.rearrange("(q p e) j -> q e p j", q=HALVES, e=2)[q, e], y[:, e, :])
 
         angles0 = gather_angles(0)
@@ -249,7 +252,7 @@ def tile_attend_gpturned_kernel(tc, tab_words, tab_scales, w1, cosn, sinn, gain,
         for e in range(2):
             turn_sum(h1, terms1, e)
         th0, m0 = activate(0, h0, "wo_raw0")
-        wo_g1 = cast_weight("wo_1", wo_raw[1], "sin_rows0")
+        wo_g1 = cast_weight("wo_1", wo_raw[1], "w1_raw0")
         th1, m1 = activate(1, h1, "wo_raw1")
         dy_q = quantise("dy", dy_grouped, J, "scs0")
         c0_0 = product(bank("c0_0", "a_c0"), dy_q, quantise("wo_0", wo_g0, HALF, "scs1"))
@@ -258,15 +261,15 @@ def tile_attend_gpturned_kernel(tc, tab_words, tab_scales, w1, cosn, sinn, gain,
         z1_0 = shifted("z1", 0, m0, MULT, z0_0)
         c0_1 = product(bank("c0_1", "a_c1"), dy_q, quantise("wo_1", wo_g1, HALF))
         z2_0 = shifted("z2", 0, th0, MULT, z1_0)
+        z3_0 = weigh(0, z2_0, sq0)
         tables0 = back_tables(0, normed0, "dy_raw")
         z0_1 = shifted("z0", 1, h1, ADD, m1)
-        z3_0 = weigh(0, z2_0, sq0)
         sq1 = lead_square(1, th1, c0_1)
-        tables1 = back_tables(1, normed1, "sin_rows0")
+        tables1 = back_tables(1, normed1, "w1_raw0")
         z1_1 = shifted("z1", 1, m1, MULT, z0_1)
         z2_1 = shifted("z2", 1, th1, MULT, z1_1)
-        ha0 = turn_back(0, z3_0, tables0)
         z3_1 = weigh(1, z2_1, sq1)
+        ha0 = turn_back(0, z3_0, tables0)
         ha1 = turn_back(1, z3_1, tables1)
-        finish(0, ha0)
+        finish(0, ha0, "z31")
         finish(1, ha1)

@@ -120,14 +120,17 @@ def tile_attend_gpturned_kernel(tc, tab_words, tab_scales, w1, cosn, sinn, gain,
             nc.vector.tensor_tensor(normed[:], scs[:, 0:2, :], norm[:].unsqueeze(1).to_broadcast([P, 2, J]), MULT)
             return normed
 
-        def back_tables(q, normed, after=None):
+        def back_tables(q, normed, after):
             table = sb("table%d" % q, [P, 2, 2, J], F32, after)
-            nc.scalar.activation(table[:, 0, 0, :], normed[:, 1, :], ACT.Copy, scale=cube[:, q, 0:1])
-            nc.scalar.activation(table[:, 0, 1, :], normed[:, 0, :], ACT.Copy, scale=neg_cube[:, q : q + 1])
-            nc.scalar.activation(table[:, 1], normed[:], ACT.Copy, scale=cube[:, q, 1:2])
+            nc.gpsimd.tensor_scalar(table[:, 0, 0, :], normed[:, 1, :], cube[:, q, 0:1], 0.0, MULT, ADD)
+            nc.gpsimd.tensor_scalar(table[:, 0, 1, :], normed[:, 0, :], neg_cube[:, q : q + 1], 0.0, MULT, ADD)
+            nc.gpsimd.tensor_scalar(table[:, 1], normed[:], cube[:, q, 1:2], 0.0, MULT, ADD)
+            return table
+
+        def turn_tables(q, table, banks):
             turned = []
             for jb in range(2):
-                dst = psum.tile([P, 2, 2, P], F32, name="table_t%d%d" % (q, jb))
+                dst = psum.tile([P, 2, 2, P], F32, name="table_t%d%d" % (q, jb), tag=banks[jb])
                 for e in range(2):
                     for to in range(2):
                         nc.tensor.transpose(dst[:, e, to, :], table[:, e, to, P * jb : P * (jb + 1)], identity[:])
@@ -172,19 +175,30 @@ def tile_attend_gpturned_kernel(tc, tab_words, tab_scales, w1, cosn, sinn, gain,
                 nc.vector.scalar_tensor_tensor(terms[:, e], a[:], half_gain[:, q, e : e + 1], planes(scs, e), MULT, MULT)
             return terms
 
-        def turn_sum(h, terms, e):
-            for jb in range(2):
-                slots = slice(P * jb, P * (jb + 1))
-                sum_turned(h[:, jb, P * e : P * (e + 1)], terms[:, e, 0, slots], terms[:, e, 1, slots])
+        def turn_sum(q, terms):
+            h = [psum.tile([P, 2, P], F32, name="h%d%d" % (q, e)) for e in range(2)]
+            for e in range(2):
+                for jb in range(2):
+                    slots = slice(P * jb, P * (jb + 1))
+                    sum_turned(h[e][:, jb, :], terms[:, e, 0, slots], terms[:, e, 1, slots])
+            return h
 
         def activate(q, h, after):
             th, m = by_slot("th", q), by_slot("m", q, after)
-            nc.scalar.activation(m[:], h[:], ACT.Silu, scale=-2.0)
-            nc.scalar.activation(th[:], h[:], ACT.Tanh)
+            for e in range(2):
+                nc.scalar.activation(m[:, :, P * e : P * (e + 1)], h[e][:], ACT.Silu, scale=-2.0)
+                nc.scalar.activation(th[:, :, P * e : P * (e + 1)], h[e][:], ACT.Tanh)
             return th, m
 
-        def lead_square(q, th, c0):
-            lead, lead_sq = by_slot("lead", q), by_slot("lead_sq", q)
+        def first_factor(q, h, m, after=None):
+            z = by_slot("z0", q, after)
+            for e in range(2):
+                cols = slice(P * e, P * (e + 1))
+                nc.vector.scalar_tensor_tensor(z[:, :, cols], h[e][:], -1.0, m[:, :, cols], ADD, ADD)
+            return z
+
+        def lead_square(q, th, c0, after=None):
+            lead, lead_sq = by_slot("lead", q, after), by_slot("lead_sq", q)
             nc.vector.scalar_tensor_tensor(lead[:], th[:], 1.0, c0[:], ADD, MULT)
             nc.scalar.activation(lead_sq[:], lead[:], ACT.Square)
             return lead_sq
@@ -196,11 +210,11 @@ def tile_attend_gpturned_kernel(tc, tab_words, tab_scales, w1, cosn, sinn, gain,
 
         def weigh(q, z2, lead_sq):
             z3 = by_slot("z3", q)
-            nc.gpsimd.tensor_tensor(z3[:], z2[:], lead_sq[:], MULT)
+            nc.vector.tensor_tensor(z3[:], z2[:], lead_sq[:], MULT)
             return z3
 
         def turn_back(q, z3, tables):
-            ha = [psum.tile([P, J], F32, name="ha%d%d" % (q, to), tag=tag % q) for to, tag in enumerate(("h_ha%d", "a_c%d"))]
+            ha = [psum.tile([P, J], F32, name="ha%d%d" % (q, to), tag=tag % q) for to, tag in enumerate(("t_ha%d", "a_c%d"))]
             for jb in range(2):
                 sent = sb("sent%d%d" % (q, jb), [P, 2, 2, P])
                 source = z3[:, jb, :].rearrange("s (e p) -> s e p", e=2)
@@ -243,33 +257,29 @@ def tile_attend_gpturned_kernel(tc, tab_words, tab_scales, w1, cosn, sinn, gain,
             dy_raw[:].rearrange("p t (b i) -> p b t i", i=4),
         )
         wo_g0 = cast_weight("wo_0", wo_raw[0], "dy_raw")
-        terms0 = turn_terms(0, a0, angles0[0], "w1_raw0")
-        h0 = bank("h0", "h_ha0")
-        for e in range(2):
-            turn_sum(h0, terms0, e)
-        terms1 = turn_terms(1, a1, angles1[0])
-        h1 = bank("h1", "h_ha1")
-        for e in range(2):
-            turn_sum(h1, terms1, e)
+        h0 = turn_sum(0, turn_terms(0, a0, angles0[0], "w1_raw0"))
+        h1 = turn_sum(1, turn_terms(1, a1, angles1[0]))
         th0, m0 = activate(0, h0, "wo_raw0")
         wo_g1 = cast_weight("wo_1", wo_raw[1], "w1_raw0")
         th1, m1 = activate(1, h1, "wo_raw1")
         dy_q = quantise("dy", dy_grouped, J, "scs0")
-        c0_0 = product(bank("c0_0", "a_c0"), dy_q, quantise("wo_0", wo_g0, HALF, "scs1"))
-        z0_0 = shifted("z0", 0, h0, ADD, m0, "dy_raw")
-        sq0 = lead_square(0, th0, c0_0)
+        c0_0 = product(bank("c0_0", "a_c0"), dy_q, quantise("wo_0", wo_g0, HALF, "half_gain"))
+        table1 = back_tables(1, normed1, "tab_bytes")
+        table0 = back_tables(0, normed0, "norm1")
+        z0_0 = first_factor(0, h0, m0, "dy_raw")
+        tables0 = turn_tables(0, table0, ("h00", "h01"))
         z1_0 = shifted("z1", 0, m0, MULT, z0_0)
         c0_1 = product(bank("c0_1", "a_c1"), dy_q, quantise("wo_1", wo_g1, HALF))
         z2_0 = shifted("z2", 0, th0, MULT, z1_0)
+        sq0 = lead_square(0, th0, c0_0, "dy_raw")
+        z0_1 = first_factor(1, h1, m1)
+        tables1 = turn_tables(1, table1, ("h10", "h11"))
         z3_0 = weigh(0, z2_0, sq0)
-        tables0 = back_tables(0, normed0, "dy_raw")
-        z0_1 = shifted("z0", 1, h1, ADD, m1)
-        sq1 = lead_square(1, th1, c0_1)
-        tables1 = back_tables(1, normed1, "w1_raw0")
         z1_1 = shifted("z1", 1, m1, MULT, z0_1)
+        sq1 = lead_square(1, th1, c0_1)
         z2_1 = shifted("z2", 1, th1, MULT, z1_1)
-        z3_1 = weigh(1, z2_1, sq1)
         ha0 = turn_back(0, z3_0, tables0)
+        z3_1 = weigh(1, z2_1, sq1)
         ha1 = turn_back(1, z3_1, tables1)
         finish(0, ha0, "z31")
         finish(1, ha1)

from contextlib import ExitStack

import concourse.mybir as mybir
from concourse.masks import make_identity

K, R, F, T, J, U = 512, 512, 512, 2048, 256, 512
FLOPS = 2 * K * R * J + 2 * F * R * J

F32 = mybir.dt.float32
BF16 = mybir.dt.bfloat16
I32 = mybir.dt.int32
U32 = mybir.dt.uint32
U16 = mybir.dt.uint16
U8 = mybir.dt.uint8
FP8X4 = mybir.dt.float8_e4m3fn_x4
MULT = mybir.AluOpType.mult
ADD = mybir.AluOpType.add
ACT = mybir.ActivationFunctionType

P = 128
PACK = 4
HALVES = 2
HALF = R // HALVES


def tile_attend_gpturned_kernel(tc, tab_words, tab_scales, w1, cosn, sinn, gain, wo, dy, og, base, offs, offs2, out):
    nc = tc.nc
    with ExitStack() as ctx:
        keep = ctx.enter_context(tc.tile_pool(name="keep", bufs=1))
        psum = ctx.enter_context(tc.psum_pool(name="psum", bufs=1))

        def sb(name, shape, dtype=F32, after=None):
            return keep.tile(shape, dtype, name=name, tag=after or name, align_bytes=64)

        def by_feature(name, q):
            return sb("%s%d" % (name, q), [P, 2, J])

        def by_slot(name, q, after=None):
            return sb("%s%d" % (name, q), [P, 2, 2 * P], F32, after)

        def bank(name, tag):
            return psum.tile([P, 2, 2 * P], F32, name=name, tag=tag)

        tab_bytes = sb("tab_bytes", [P, T], U8)
        nc.vector.memset(tab_bytes[:].bitcast(I32), 0)
        warm_in = sb("warm_in", [P, 1])
        warm_out = sb("warm_out", [P, 1])
        nc.gpsimd.memset(warm_in[:], 0.0)
        nc.scalar.activation(warm_out[:], warm_in[:], ACT.Silu)
        identity = sb("identity", [P, P])
        make_identity(nc, identity[:])

        col_list = keep.tile([P, J // 16], U16, name="col_list")
        angle_list = keep.tile([P, J // 16], U16, name="angle_list")
        tab_codes = sb("tab_codes", [P, T], U32)
        gains = sb("gains", [P, HALVES, 2])
        out_gains = sb("out_gains", [P, HALVES, 2])
        dy_raw = sb("dy_raw", [P, PACK, J])

        def load_weight_half(name, w, q):
            raw = sb("%s%d" % (name, q), [P, PACK, HALF])
            nc.sync.dma_start(raw[:], w.rearrange("(p t) r -> p t r", t=PACK)[:, :, HALF * q : HALF * (q + 1)])
            return raw

        def load_angle_rows(name, table, q):
            rows = sb("%s%d" % (name, q), [P, U])
            nc.sync.dma_start(rows[:], table.rearrange("(q p e) u -> q e p u", q=HALVES, e=2)[q, 0])
            return rows

        def load_base(q):
            rows = by_feature("base_rows", q)
            nc.sync.dma_start(rows[:], base.rearrange("(q p e) j -> q p e j", q=HALVES, e=2)[q])
            return rows

        nc.sync.dma_start(angle_list[:], offs2)
        cos_rows, sin_rows = [], []
        sin_rows.append(load_angle_rows("sin_rows", sinn, 0))
        cos_rows.append(load_angle_rows("cos_rows", cosn, 0))
        sin_rows.append(load_angle_rows("sin_rows", sinn, 1))
        cos_rows.append(load_angle_rows("cos_rows", cosn, 1))
        w1_raw = [load_weight_half("w1_raw", w1, 0)]
        nc.sync.dma_start(col_list[:], offs)
        for quad in range(4):
            nc.sync.dma_start(
                tab_bytes[32 * quad : 32 * quad + 4, :].bitcast(I32),
                tab_scales[0, 4 * quad : 4 * quad + 4, :].bitcast(I32),
            )
        nc.sync.dma_start(tab_codes[:].bitcast(I32), tab_words[0].rearrange("p n t -> p (n t)").bitcast(I32))
        nc.sync.dma_start(gains[:], gain.rearrange("(q p e) o -> p q (e o)", q=HALVES, e=2))
        w1_raw.append(load_weight_half("w1_raw", w1, 1))
        nc.sync.dma_start(dy_raw[:], dy.rearrange("(p t) j -> p t j", t=PACK))
        wo_raw = [load_weight_half("wo_raw", wo, q) for q in range(HALVES)]
        nc.sync.dma_start(out_gains[:], og.rearrange("(q p e) o -> p q (e o)", q=HALVES, e=2))
        base_rows = [load_base(q) for q in range(HALVES)]

        half_gain = sb("half_gain", [P, HALVES, 2])
        gain_sq = sb("gain_sq", [P, HALVES, 2])
        cube = sb("cube", [P, HALVES, 2])
        neg_cube = sb("neg_cube", [P, HALVES])

        def gather_angles(q, after=None):
            scs = sb("scs%d" % q, [P, 3, J], F32, after)
            nc.vector.tensor_copy(scs[:, 0, :], sin_rows[q][:].indirect(angle_list[:]))
            nc.vector.tensor_copy(scs[:, 1, :], cos_rows[q][:].indirect(angle_list[:]))
            squares = by_feature("squares", q)
            nc.scalar.activation(scs[:, 2, :], scs[:, 0, :], ACT.Copy, scale=-1.0)
            nc.scalar.activation(squares[:], scs[:, 0:2, :], ACT.Square)
            return scs, squares

        def planes(scs, e):
            return scs[:, 1 - e : 3 - e, :]

        def angle_norm(q, squares):
            norm = sb("norm%d" % q, [P, J])
            nc.vector.tensor_tensor(norm[:], squares[:, 0, :], squares[:, 1, :], ADD)
            return norm

        def normed_angles(q, scs, norm, after):
            normed = sb("normed%d" % q, [P, 2, J], F32, after)
            nc.vector.tensor_tensor(normed[:], scs[:, 0:2, :], norm[:].unsqueeze(1).to_broadcast([P, 2, J]), MULT)
            return normed

        def back_tables(q, normed, after):
            table = sb("table%d" % q, [P, 2, 2, J], F32, after)
            nc.gpsimd.tensor_scalar(table[:, 0, 0, :], normed[:, 1, :], cube[:, q, 0:1], 0.0, MULT, ADD)
            nc.gpsimd.tensor_scalar(table[:, 0, 1, :], normed[:, 0, :], neg_cube[:, q : q + 1], 0.0, MULT, ADD)
            nc.gpsimd.tensor_scalar(table[:, 1], normed[:], cube[:, q, 1:2], 0.0, MULT, ADD)
            return table

        def turn_tables(q, table, banks):
            turned = []
            for jb in range(2):
                dst = psum.tile([P, 2, 2, P], F32, name="table_t%d%d" % (q, jb), tag=banks[jb])
                for e in range(2):
                    for to in range(2):
                        nc.tensor.transpose(dst[:, e, to, :], table[:, e, to, P * jb : P * (jb + 1)], identity[:])
                turned.append(dst)
            return turned

        def quantise(name, grouped, width, after=None):
            codes = sb(name + "_codes", [P, width], U32, after)
            scales = sb(name + "_scales", [P, width], U8)
            nc.vector.quantize_mx(out=codes[:].bitcast(FP8X4), scales=scales[:], in_=grouped[:])
            return codes, scales

        def cast_weight(name, raw, after):
            grouped = sb(name + "_grouped", [P, HALF * PACK], BF16, after)
            nc.scalar.copy(
                grouped[:].rearrange("p (e b i t) -> p b t i e", e=2, i=2, t=PACK),
                raw[:].rearrange("p t (b i e) -> p b t i e", i=2, e=2),
            )
            return grouped

        def product(acc, stationary, moving):
            for block in range(2):
                cols = slice(P * block, P * (block + 1))
                nc.tensor.matmul_mx(
                    out=acc[:, block, :],
                    lhsT=stationary[0][:, cols].bitcast(FP8X4),
                    lhsT_scale=stationary[1][:, cols],
                    rhs=moving[0][:].bitcast(FP8X4),
                    rhs_scale=moving[1][:],
                    start=True,
                    stop=True,
                )
            return acc

        def sum_turned(dst, first, second):
            nc.tensor.matmul(dst, first, identity[:], start=True, stop=False, is_transpose=True)
            nc.tensor.matmul(dst, second, identity[:], start=False, stop=True, is_transpose=True)

        def turn_terms(q, a, scs, after=None):
            terms = sb("terms%d" % q, [P, 2, 2, J], F32, after)
            for e in range(2):
                nc.vector.scalar_tensor_tensor(terms[:, e], a[:], half_gain[:, q, e : e + 1], planes(scs, e), MULT, MULT)
            return terms

        def turn_sum(q, terms):
            h = [psum.tile([P, 2, P], F32, name="h%d%d" % (q, e)) for e in range(2)]
            for e in range(2):
                for jb in range(2):
                    slots = slice(P * jb, P * (jb + 1))
                    sum_turned(h[e][:, jb, :], terms[:, e, 0, slots], terms[:, e, 1, slots])
            return h

        def activate(q, h, after):
            th, m = by_slot("th", q), by_slot("m", q, after)
            for e in range(2):
                nc.scalar.activation(m[:, :, P * e : P * (e + 1)], h[e][:], ACT.Silu, scale=-2.0)
                nc.scalar.activation(th[:, :, P * e : P * (e + 1)], h[e][:], ACT.Tanh)
            return th, m

        def first_factor(q, h, m, after=None):
            z = by_slot("z0", q, after)
            for e in range(2):
                cols = slice(P * e, P * (e + 1))
                nc.vector.scalar_tensor_tensor(z[:, :, cols], h[e][:], -1.0, m[:, :, cols], ADD, ADD)
            return z

        def lead_square(q, th, c0, after=None):
            lead, lead_sq = by_slot("lead", q, after), by_slot("lead_sq", q)
            nc.vector.scalar_tensor_tensor(lead[:], th[:], 1.0, c0[:], ADD, MULT)
            nc.scalar.activation(lead_sq[:], lead[:], ACT.Square)
            return lead_sq

        def shifted(name, q, first, op, second, after=None):
            z = by_slot(name, q, after)
            nc.vector.scalar_tensor_tensor(z[:], first[:], -1.0, second[:], ADD, op)
            return z

        def weigh(q, z2, lead_sq):
            z3 = by_slot("z3", q)
            nc.vector.tensor_tensor(z3[:], z2[:], lead_sq[:], MULT)
            return z3

        def turn_back(q, z3, tables):
            ha = [psum.tile([P, J], F32, name="ha%d%d" % (q, to), tag=tag % q) for to, tag in enumerate(("t_ha%d", "a_c%d"))]
            for jb in range(2):
                sent = sb("sent%d%d" % (q, jb), [P, 2, 2, P])
                source = z3[:, jb, :].rearrange("s (e p) -> s e p", e=2)
                if jb == 0:
                    nc.vector.tensor_tensor(sent[:], tables[jb][:], source.unsqueeze(2).to_broadcast([P, 2, 2, P]), MULT)
                for to in range(2):
                    if jb == 1:
                        nc.vector.tensor_tensor(sent[:, :, to, :], tables[jb][:, :, to, :], source, MULT)
                    sum_turned(ha[to][:, P * jb : P * (jb + 1)], sent[:, 0, to, :], sent[:, 1, to, :])
            return ha

        def finish(q, ha, after=None):
            y = sb("y%d" % q, [P, 2, J], F32, after)
            for e in range(2):
                nc.vector.scalar_tensor_tensor(y[:, e, :], ha[e][:], out_gains[:, q, e : e + 1], base_rows[q][:, e, :], MULT, ADD)
                nc.sync.dma_start(out.rearrange("(q p e) j -> q e p j", q=HALVES, e=2)[q, e], y[:, e, :])

        angles0 = gather_angles(0)
        angles1 = gather_angles(1)
        norm0 = angle_norm(0, angles0[1])
        w1_g0 = cast_weight("w1_0", w1_raw[0], "cos_rows1")
        tab_gs = sb("tab_gs", [P, J], U8, "squares0")
        nc.vector.tensor_copy(tab_gs[:], tab_bytes[:].indirect(col_list[:]))
        norm1 = angle_norm(1, angles1[1])
        w1_q0 = quantise("w1_0", w1_g0, HALF, "tab_bytes")
        tab_g = sb("tab_g", [P, J], U32, "squares1")
        nc.vector.tensor_copy(tab_g[:], tab_codes[:].indirect(col_list[:]))
        a0 = product(bank("a0", "a_c0"), w1_q0, (tab_g, tab_gs))
        nc.scalar.activation(half_gain[:], gains[:], ACT.Copy, scale=0.5)
        nc.scalar.activation(gain_sq[:], gains[:], ACT.Square)
        normed0 = normed_angles(0, angles0[0], norm0, "tab_codes")
        normed1 = normed_angles(1, angles1[0], norm1, "norm0")
        nc.vector.scalar_tensor_tensor(cube[:], gain_sq[:], -0.5, gains[:], MULT, MULT)
        nc.vector.scalar_tensor_tensor(neg_cube[:], gain_sq[:, :, 0], 0.5, gains[:, :, 0], MULT, MULT)
        w1_g1 = cast_weight("w1_1", w1_raw[1], "w1_raw0")
        a1 = product(bank("a1", "a_c1"), quantise("w1_1", w1_g1, HALF, "norm1"), (tab_g, tab_gs))
        dy_grouped = sb("dy_grouped", [P, J * PACK], BF16, "w1_raw1")
        nc.scalar.copy(
            dy_grouped[:].rearrange("p (b i t) -> p b t i", i=4, t=PACK),
            dy_raw[:].rearrange("p t (b i) -> p b t i", i=4),
        )
        wo_g0 = cast_weight("wo_0", wo_raw[0], "dy_raw")
        h0 = turn_sum(0, turn_terms(0, a0, angles0[0], "w1_raw0"))
        h1 = turn_sum(1, turn_terms(1, a1, angles1[0]))
        th0, m0 = activate(0, h0, "wo_raw0")
        wo_g1 = cast_weight("wo_1", wo_raw[1], "w1_raw0")
        th1, m1 = activate(1, h1, "wo_raw1")
        dy_q = quantise("dy", dy_grouped, J, "scs0")
        c0_0 = product(bank("c0_0", "a_c0"), dy_q, quantise("wo_0", wo_g0, HALF, "half_gain"))
        table1 = back_tables(1, normed1, "tab_bytes")
        table0 = back_tables(0, normed0, "norm1")
        z0_0 = first_factor(0, h0, m0, "dy_raw")
        tables0 = turn_tables(0, table0, ("h00", "h01"))
        z1_0 = shifted("z1", 0, m0, MULT, z0_0)
        c0_1 = product(bank("c0_1", "a_c1"), dy_q, quantise("wo_1", wo_g1, HALF))
        z2_0 = shifted("z2", 0, th0, MULT, z1_0)
        sq0 = lead_square(0, th0, c0_0, "dy_raw")
        z0_1 = first_factor(1, h1, m1)
        tables1 = turn_tables(1, table1, ("h10", "h11"))
        z3_0 = weigh(0, z2_0, sq0)
        z1_1 = shifted("z1", 1, m1, MULT, z0_1)
        sq1 = lead_square(1, th1, c0_1)
        z2_1 = shifted("z2", 1, th1, MULT, z1_1)
        ha0 = turn_back(0, z3_0, tables0)
        z3_1 = weigh(1, z2_1, sq1)
        ha1 = turn_back(1, z3_1, tables1)
        finish(0, ha0, "z31")
        finish(1, ha1)
